import numpy as np, ml_dtypes
CORES = [24,48,72,152,176,200]
N = 6
CB = 128
def setup_inputs(rng):
    return {"x": rng.standard_normal((N, 128, N * CB), dtype=np.float32).astype(ml_dtypes.bfloat16)}
def setup_inputs_big(rng):
    d = setup_inputs(rng)
    for k in ("x",): d[k] = (d[k].astype(np.float32) * 1024.0).astype(d[k].dtype)
    return d
def setup_inputs_small(rng):
    d = setup_inputs(rng)
    for k in ("x",): d[k] = (d[k].astype(np.float32) * (1 / 1024.0)).astype(d[k].dtype)
    return d
def setup_inputs_apart(rng):
    d = setup_inputs(rng)
    f = (10.0 ** rng.permutation(np.linspace(-1.5, 1.5, N))).astype(np.float32).reshape(N, 1, 1)
    for k in ("x",): d[k] = (d[k].astype(np.float32) * f).astype(d[k].dtype)
    return d
def reference(x):
    X = x.astype(np.float64)
    G = sum(X[j].T @ X[j] for j in range(N))
    y = np.full((N, CB, N * CB), np.nan)
    for r in range(N):
        y[r][:, :CB * r] = G[CB * r:CB * r + CB, :CB * r]
    return {"y": y.astype(ml_dtypes.bfloat16 if x.dtype != np.float64 else np.float64)}

@@ -1,0 +1,170 @@
+from concourse.bass import DstId, RemoteDMATransfer
+
+N = 6
+CB = 128
+W = N * CB
+
+SCRATCH = {
+    "land": ("sbuf", [128, N * W], "bfloat16"),
+    "ysb": ("sbuf", [128, (N - 1) * CB], "bfloat16"),
+    "ps0": ("psum", [128, 512], "float32"),
+    "ps1": ("psum", [128, 512], "float32"),
+}
+SEMAPHORES = ["ld", "sent", "hub", "a0", "a1", "a2", "a3", "a4", "a5", "mm0", "mm1", "ev0", "ev1", "st"]
+
+_CACHE = {}
+
+
+def _nbits(m):
+    return bin(m).count("1")
+
+
+def _plan(T, topo):
+    if "p" in _CACHE:
+        return _CACHE["p"]
+    cores = list(T.cores)
+    n = len(cores)
+    world = (max(topo.host(c) for c in cores) + 1) * topo.CORES_PER_HOST
+    onchip = {}
+    sends = {}
+    hub_of = {}
+    kind = {}
+    for j, cj in enumerate(cores):
+        mine = [c for c in range(world)
+                if c != cj and topo.host(c) == topo.host(cj) and topo.chip(c) == topo.chip(cj)]
+        dests = [r for r in range(n - 1, 0, -1) if r != j]
+        direct = [r for r in dests if topo.may_write(cj, cores[r])]
+        cross = [r for r in dests if not topo.may_write(cj, cores[r])]
+        sends[cj] = [(j, r, 0, CB * (r + 1)) for r in direct]
+        for k, r in enumerate(direct):
+            kind[(j, r)] = (0, k)
+        onchip[cj] = []
+        if not cross:
+            continue
+        port = [c for c in mine if all(topo.may_write(c, cores[r]) for r in cross)]
+        near = [c for c in port if topo.die(c) == topo.die(cj)]
+        far = [c for c in port if topo.die(c) != topo.die(cj)]
+        big = cross[0]
+        nd = sum(1 for i in range(n) if i != big and topo.may_write(cores[i], cores[big]))
+        if nd > n - 1 - nd:
+            pair, spare = far[:2], near + far[2:]
+        else:
+            pair, spare = [near[0], far[0]], near[1:] + far[1:]
+        w = CB * (big + 1)
+        hold = [(0, w // 2), (w // 2, w)]
+        onchip[cj].append([(pair[k], hold[k][0], hold[k][1]) for k in range(2)])
+        for k in range(2):
+            sends[pair[k]] = []
+            hub_of[pair[k]] = j
+        for p, r in enumerate(cross[:2]):
+            kind[(j, r)] = (1, p)
+            for k in range(2):
+                a, b = hold[k][0], min(hold[k][1], CB * (r + 1))
+                if b > a:
+                    sends[pair[k]].append((j, r, a, b))
+        for i, r in enumerate(cross[2:]):
+            c = spare[i]
+            hub_of[c] = j
+            kind[(j, r)] = (1, 1 + i)
+            onchip[cj].append([(c, 0, CB * (r + 1))])
+            sends[c] = [(j, r, 0, CB * (r + 1))]
+    expect = {}
+    for s, lst in sends.items():
+        for (j, r, a, b) in lst:
+            expect[(r, j)] = expect.get((r, j), 0) + _nbits(topo.mask(s, cores[r]))
+    p = {"cores": cores, "onchip": onchip, "sends": sends, "hub_of": hub_of, "kind": kind, "expect": expect}
+    _CACHE["p"] = p
+    return p
+
+
+def _send_all(g, core, T, topo, P):
+    tot = 0
+    for (j, r, a, b) in P["sends"].get(core, []):
+        d = P["cores"][r]
+        rid, pid = topo.addr(d, core)
+        m = topo.mask(core, d)
+        ap = T.land[:, j * W + a:j * W + b]
+        g.remote_dma(out_ap=ap, in_ap=ap, remote_sem=T.sem["a%d" % j], local_sem=T.sem.sent,
+                     pid=pid, routing_id=rid, dma_engine_mask=m)
+        tot += _nbits(m)
+    return tot
+
+
+def rank_program(g, core, T, topo):
+    P = _plan(T, topo)
+    rank = T.rank_of(core)
+
+    if rank is None:
+        if core not in P["hub_of"]:
+            return
+        src = P["cores"][P["hub_of"][core]]
+        got = 0
+        for call in P["onchip"][src]:
+            masks = _onchip_masks(topo, P, src, call)
+            for (h, a, b), m in zip(call, masks):
+                if h == core:
+                    got += _nbits(m)
+        g.wait_ge(T.sem.hub, got)
+        tot = _send_all(g, core, T, topo, P)
+        g.wait_ge(T.sem.sent, tot)
+        return
+
+    j = rank
+    g.sync.dma_start(T.land[:, j * W:(j + 1) * W], T.x[:, :]).then_inc(T.sem.ld, 16)
+
+    g.wait_ge(T.sem.ld, 16)
+    tot = 0
+    for call in P["onchip"][core]:
+        masks = _onchip_masks(topo, P, core, call)
+        trs = []
+        for (h, a, b), m in zip(call, masks):
+            rid, pid = topo.addr(h, core)
+            ap = T.land[:, j * W + a:j * W + b]
+            trs.append(RemoteDMATransfer(dst_ids=[DstId(rid=rid, pnc=pid)], dma_engine_mask=m,
+                                         remote_sem=T.sem.hub, src=ap, dst=ap))
+            tot += _nbits(m)
+        g.remote_dma_fused(trs, local_sem=T.sem.sent)
+    tot += _send_all(g, core, T, topo, P)
+
+    r = rank
+    nst = 0
+    if r >= 1:
+        wid = CB * r
+        if r >= 3:
+            chunks = [(0, wid // 2), (wid // 2, wid)]
+        else:
+            chunks = [(0, wid)]
+        others = sorted([i for i in range(len(P["cores"])) if i != r], key=lambda i: P["kind"][(i, r)])
+        order = [r] + others
+        for n_, i in enumerate(order):
+            if i == r:
+                g.tensor.wait_ge(T.sem.ld, 16)
+            else:
+                g.tensor.wait_ge(T.sem["a%d" % i], P["expect"][(r, i)])
+            lhsT = T.land[:, i * W + r * CB:i * W + (r + 1) * CB]
+            for k, (a, b) in enumerate(chunks):
+                g.tensor.matmul(T["ps%d" % k][:, 0:b - a], lhsT, T.land[:, i * W + a:i * W + b],
+                                n_ == 0, n_ == len(order) - 1).then_inc(T.sem["mm%d" % k], 1)
+        for k, (a, b) in enumerate(chunks):
+            g.vector.wait_ge(T.sem["mm%d" % k], len(order))
+            g.vector.tensor_copy(T.ysb[:, a:b], T["ps%d" % k][:, 0:b - a]).then_inc(T.sem["ev%d" % k], 1)
+        for k, (a, b) in enumerate(chunks):
+            q = g.sync if k == 0 else g.scalar
+            q.wait_ge(T.sem["ev%d" % k], 1)
+            q.dma_start(T.y[:, a:b], T.ysb[:, a:b]).then_inc(T.sem.st, 16)
+            nst += 16
+
+    g.wait_ge(T.sem.sent, tot)
+    if nst:
+        g.wait_ge(T.sem.st, nst)
+
+
+def _onchip_masks(topo, P, src, call):
+    full = topo.mask(src, call[0][0])
+    off = full
+    for (j, r, a, b) in P["sends"].get(src, []):
+        off = off & topo.mask(src, P["cores"][r])
+    lo, hi = full & off, full & ~off
+    if len(call) == 2:
+        return [lo, hi]
+    return [hi]

@@ -19,60 +19,91 @@ def _nbits(m):
     return bin(m).count("1")
 
 
+def _mate_hub(topo, world, cj, db, place):
+    mh = [c for c in range(world) if topo.mates(c, db) and topo.may_write(c, db) and topo.may_write(cj, c)]
+    dies = sorted(set(topo.die(c) for c in mh), reverse=True)
+    return [c for c in mh if topo.die(c) == dies[place % len(dies)]][0]
+
+
 def _plan(T, topo):
     if "p" in _CACHE:
         return _CACHE["p"]
     cores = list(T.cores)
     n = len(cores)
     world = (max(topo.host(c) for c in cores) + 1) * topo.CORES_PER_HOST
-    onchip = {}
+    feed = {}
     sends = {}
     hub_of = {}
-    kind = {}
+    most = max(sum(1 for r in range(1, n) if r != j and topo.may_write(cores[j], cores[r])) for j in range(n))
     for j, cj in enumerate(cores):
         mine = [c for c in range(world)
                 if c != cj and topo.host(c) == topo.host(cj) and topo.chip(c) == topo.chip(cj)]
         dests = [r for r in range(n - 1, 0, -1) if r != j]
         direct = [r for r in dests if topo.may_write(cj, cores[r])]
         cross = [r for r in dests if not topo.may_write(cj, cores[r])]
-        sends[cj] = [(j, r, 0, CB * (r + 1)) for r in direct]
-        for k, r in enumerate(direct):
-            kind[(j, r)] = (0, k)
-        onchip[cj] = []
-        if not cross:
-            continue
+        give = []
+        if sum(CB * (r + 1) for r in direct) > W + W // 2:
+            give = [direct[1]]
+        keep = [r for r in direct if r not in give]
+        if len(direct) == most:
+            keep = keep[::-1]
+        sends[cj] = [(j, r, 0, CB * (r + 1)) for r in keep]
+        feed[cj] = []
         port = [c for c in mine if all(topo.may_write(c, cores[r]) for r in cross)]
         near = [c for c in port if topo.die(c) == topo.die(cj)]
         far = [c for c in port if topo.die(c) != topo.die(cj)]
         big = cross[0]
-        nd = sum(1 for i in range(n) if i != big and topo.may_write(cores[i], cores[big]))
-        if nd > n - 1 - nd:
-            pair, spare = far[:2], near + far[2:]
-        else:
-            pair, spare = [near[0], far[0]], near[1:] + far[1:]
+        peers = [i for i in range(n) if not topo.may_write(cores[i], cores[big])]
+        place = peers.index(j)
         w = CB * (big + 1)
-        hold = [(0, w // 2), (w // 2, w)]
-        onchip[cj].append([(pair[k], hold[k][0], hold[k][1]) for k in range(2)])
-        for k in range(2):
-            sends[pair[k]] = []
-            hub_of[pair[k]] = j
-        for p, r in enumerate(cross[:2]):
-            kind[(j, r)] = (1, p)
+        if len(cross) == 2:
+            spare = [near[1], far[1]]
+            hold = [(0, w // 2), (w // 2, w)]
+            early = place < len(peers) // 2
+            if early:
+                pair = [near[0], far[0]]
+                feed[cj].append([(pair[k], hold[k][0], hold[k][1]) for k in range(2)])
+            else:
+                pair = [near[0] if place % 2 == 0 else far[0], _mate_hub(topo, world, cj, cores[big], place)]
+                for k in range(2):
+                    feed[cj].append([(pair[k], hold[k][0], hold[k][1])])
             for k in range(2):
-                a, b = hold[k][0], min(hold[k][1], CB * (r + 1))
-                if b > a:
-                    sends[pair[k]].append((j, r, a, b))
-        for i, r in enumerate(cross[2:]):
-            c = spare[i]
-            hub_of[c] = j
-            kind[(j, r)] = (1, 1 + i)
-            onchip[cj].append([(c, 0, CB * (r + 1))])
-            sends[c] = [(j, r, 0, CB * (r + 1))]
+                sends[pair[k]] = []
+                hub_of[pair[k]] = j
+            two = cross[::-1] if early else cross
+            for r in two:
+                for k in range(2):
+                    a, b = hold[k][0], min(hold[k][1], CB * (r + 1))
+                    if b > a:
+                        sends[pair[k]].append((j, r, a, b))
+            for r in give:
+                c = spare[0]
+                hub_of[c] = j
+                feed[cj].append([(c, 0, CB * (r + 1))])
+                sends[c] = [(j, r, 0, CB * (r + 1))]
+            if not give and n - 1 in direct:
+                c = spare[1]
+                hub_of[c] = j
+                feed[cj].append([(c, W // 2, W)])
+                sends[c] = [(j, n - 1, W // 2, W)]
+                sends[cj] = [(j, r, 0, min(CB * (r + 1), W // 2)) for r in keep]
+        else:
+            m_ = _mate_hub(topo, world, cj, cores[big], place)
+            todo = [(far[0], big, 0, w // 2), (m_, big, w // 2, w),
+                    (far[1], cross[1], 0, CB * (cross[1] + 1)), (near[0], cross[2], 0, CB * (cross[2] + 1))]
+            for (c, r, a, b) in todo:
+                hub_of[c] = j
+                feed[cj].append([(c, a, b)])
+                sends[c] = [(j, r, a, b)]
     expect = {}
+    due = {}
     for s, lst in sends.items():
+        ahead = 0 if s in cores else 2 * W
         for (j, r, a, b) in lst:
+            ahead += b - a
             expect[(r, j)] = expect.get((r, j), 0) + _nbits(topo.mask(s, cores[r]))
-    p = {"cores": cores, "onchip": onchip, "sends": sends, "hub_of": hub_of, "kind": kind, "expect": expect}
+            due[(r, j)] = max(due.get((r, j), 0), ahead)
+    p = {"cores": cores, "feed": feed, "sends": sends, "hub_of": hub_of, "due": due, "expect": expect}
     _CACHE["p"] = p
     return p
 
@@ -90,6 +121,19 @@ def _send_all(g, core, T, topo, P):
     return tot
 
 
+def _hub_masks(topo, P, src, call):
+    full = topo.mask(src, call[0][0])
+    off = full
+    for (j, r, a, b) in P["sends"].get(src, []):
+        off = off & topo.mask(src, P["cores"][r])
+    lo, hi = full & off, full & ~off
+    if len(call) == 2:
+        return [lo, hi]
+    if hi:
+        return [hi]
+    return [full]
+
+
 def rank_program(g, core, T, topo):
     P = _plan(T, topo)
     rank = T.rank_of(core)
@@ -99,8 +143,8 @@ def rank_program(g, core, T, topo):
             return
         src = P["cores"][P["hub_of"][core]]
         got = 0
-        for call in P["onchip"][src]:
-            masks = _onchip_masks(topo, P, src, call)
+        for call in P["feed"][src]:
+            masks = _hub_masks(topo, P, src, call)
             for (h, a, b), m in zip(call, masks):
                 if h == core:
                     got += _nbits(m)
@@ -114,8 +158,8 @@ def rank_program(g, core, T, topo):
 
     g.wait_ge(T.sem.ld, 16)
     tot = 0
-    for call in P["onchip"][core]:
-        masks = _onchip_masks(topo, P, core, call)
+    for call in P["feed"][core]:
+        masks = _hub_masks(topo, P, core, call)
         trs = []
         for (h, a, b), m in zip(call, masks):
             rid, pid = topo.addr(h, core)
@@ -134,7 +178,7 @@ def rank_program(g, core, T, topo):
             chunks = [(0, wid // 2), (wid // 2, wid)]
         else:
             chunks = [(0, wid)]
-        others = sorted([i for i in range(len(P["cores"])) if i != r], key=lambda i: P["kind"][(i, r)])
+        others = sorted([i for i in range(len(P["cores"])) if i != r], key=lambda i: P["due"][(r, i)])
         order = [r] + others
         for n_, i in enumerate(order):
             if i == r:
@@ -157,14 +201,3 @@ def rank_program(g, core, T, topo):
     g.wait_ge(T.sem.sent, tot)
     if nst:
         g.wait_ge(T.sem.st, nst)
-
-
-def _onchip_masks(topo, P, src, call):
-    full = topo.mask(src, call[0][0])
-    off = full
-    for (j, r, a, b) in P["sends"].get(src, []):
-        off = off & topo.mask(src, P["cores"][r])
-    lo, hi = full & off, full & ~off
-    if len(call) == 2:
-        return [lo, hi]
-    return [hi]

from concourse.bass import DstId, RemoteDMATransfer

N = 6
CB = 128
W = N * CB

SCRATCH = {
    "land": ("sbuf", [128, N * W], "bfloat16"),
    "ysb": ("sbuf", [128, (N - 1) * CB], "bfloat16"),
    "ps0": ("psum", [128, 512], "float32"),
    "ps1": ("psum", [128, 512], "float32"),
}
SEMAPHORES = ["ld", "sent", "hub", "a0", "a1", "a2", "a3", "a4", "a5", "mm0", "mm1", "ev0", "ev1", "st"]

_CACHE = {}


def _nbits(m):
    return bin(m).count("1")


def _mate_hub(topo, world, cj, db, place):
    mh = [c for c in range(world) if topo.mates(c, db) and topo.may_write(c, db) and topo.may_write(cj, c)]
    dies = sorted(set(topo.die(c) for c in mh), reverse=True)
    return [c for c in mh if topo.die(c) == dies[place % len(dies)]][0]


def _plan(T, topo):
    if "p" in _CACHE:
        return _CACHE["p"]
    cores = list(T.cores)
    n = len(cores)
    world = (max(topo.host(c) for c in cores) + 1) * topo.CORES_PER_HOST
    feed = {}
    sends = {}
    hub_of = {}
    most = max(sum(1 for r in range(1, n) if r != j and topo.may_write(cores[j], cores[r])) for j in range(n))
    for j, cj in enumerate(cores):
        mine = [c for c in range(world)
                if c != cj and topo.host(c) == topo.host(cj) and topo.chip(c) == topo.chip(cj)]
        dests = [r for r in range(n - 1, 0, -1) if r != j]
        direct = [r for r in dests if topo.may_write(cj, cores[r])]
        cross = [r for r in dests if not topo.may_write(cj, cores[r])]
        give = []
        if sum(CB * (r + 1) for r in direct) > W + W // 2:
            give = [direct[1]]
        keep = [r for r in direct if r not in give]
        if len(direct) == most:
            keep = keep[::-1]
        sends[cj] = [(j, r, 0, CB * (r + 1)) for r in keep]
        feed[cj] = []
        port = [c for c in mine if all(topo.may_write(c, cores[r]) for r in cross)]
        near = [c for c in port if topo.die(c) == topo.die(cj)]
        far = [c for c in port if topo.die(c) != topo.die(cj)]
        big = cross[0]
        peers = [i for i in range(n) if not topo.may_write(cores[i], cores[big])]
        place = peers.index(j)
        w = CB * (big + 1)
        if len(cross) == 2:
            spare = [near[1], far[1]]
            hold = [(0, w // 2), (w // 2, w)]
            early = place < len(peers) // 2
            if early:
                pair = [near[0], far[0]]
                feed[cj].append([(pair[k], hold[k][0], hold[k][1]) for k in range(2)])
            else:
                pair = [near[0] if place % 2 == 0 else far[0], _mate_hub(topo, world, cj, cores[big], place)]
                for k in range(2):
                    feed[cj].append([(pair[k], hold[k][0], hold[k][1])])
            for k in range(2):
                sends[pair[k]] = []
                hub_of[pair[k]] = j
            two = cross[::-1] if early else cross
            for r in two:
                for k in range(2):
                    a, b = hold[k][0], min(hold[k][1], CB * (r + 1))
                    if b > a:
                        sends[pair[k]].append((j, r, a, b))
            for r in give:
                c = spare[0]
                hub_of[c] = j
                feed[cj].append([(c, 0, CB * (r + 1))])
                sends[c] = [(j, r, 0, CB * (r + 1))]
            if not give and n - 1 in direct:
                c = spare[1]
                hub_of[c] = j
                feed[cj].append([(c, W // 2, W)])
                sends[c] = [(j, n - 1, W // 2, W)]
                sends[cj] = [(j, r, 0, min(CB * (r + 1), W // 2)) for r in keep]
        else:
            m_ = _mate_hub(topo, world, cj, cores[big], place)
            todo = [(far[0], big, 0, w // 2), (m_, big, w // 2, w),
                    (far[1], cross[1], 0, CB * (cross[1] + 1)), (near[0], cross[2], 0, CB * (cross[2] + 1))]
            for (c, r, a, b) in todo:
                hub_of[c] = j
                feed[cj].append([(c, a, b)])
                sends[c] = [(j, r, a, b)]
    expect = {}
    due = {}
    for s, lst in sends.items():
        ahead = 0 if s in cores else 2 * W
        for (j, r, a, b) in lst:
            ahead += b - a
            expect[(r, j)] = expect.get((r, j), 0) + _nbits(topo.mask(s, cores[r]))
            due[(r, j)] = max(due.get((r, j), 0), ahead)
    p = {"cores": cores, "feed": feed, "sends": sends, "hub_of": hub_of, "due": due, "expect": expect}
    _CACHE["p"] = p
    return p


def _send_all(g, core, T, topo, P):
    tot = 0
    for (j, r, a, b) in P["sends"].get(core, []):
        d = P["cores"][r]
        rid, pid = topo.addr(d, core)
        m = topo.mask(core, d)
        ap = T.land[:, j * W + a:j * W + b]
        g.remote_dma(out_ap=ap, in_ap=ap, remote_sem=T.sem["a%d" % j], local_sem=T.sem.sent,
                     pid=pid, routing_id=rid, dma_engine_mask=m)
        tot += _nbits(m)
    return tot


def _hub_masks(topo, P, src, call):
    full = topo.mask(src, call[0][0])
    off = full
    for (j, r, a, b) in P["sends"].get(src, []):
        off = off & topo.mask(src, P["cores"][r])
    lo, hi = full & off, full & ~off
    if len(call) == 2:
        return [lo, hi]
    if hi:
        return [hi]
    return [full]


def rank_program(g, core, T, topo):
    P = _plan(T, topo)
    rank = T.rank_of(core)

    if rank is None:
        if core not in P["hub_of"]:
            return
        src = P["cores"][P["hub_of"][core]]
        got = 0
        for call in P["feed"][src]:
            masks = _hub_masks(topo, P, src, call)
            for (h, a, b), m in zip(call, masks):
                if h == core:
                    got += _nbits(m)
        g.wait_ge(T.sem.hub, got)
        tot = _send_all(g, core, T, topo, P)
        g.wait_ge(T.sem.sent, tot)
        return

    j = rank
    g.sync.dma_start(T.land[:, j * W:(j + 1) * W], T.x[:, :]).then_inc(T.sem.ld, 16)

    g.wait_ge(T.sem.ld, 16)
    tot = 0
    for call in P["feed"][core]:
        masks = _hub_masks(topo, P, core, call)
        trs = []
        for (h, a, b), m in zip(call, masks):
            rid, pid = topo.addr(h, core)
            ap = T.land[:, j * W + a:j * W + b]
            trs.append(RemoteDMATransfer(dst_ids=[DstId(rid=rid, pnc=pid)], dma_engine_mask=m,
                                         remote_sem=T.sem.hub, src=ap, dst=ap))
            tot += _nbits(m)
        g.remote_dma_fused(trs, local_sem=T.sem.sent)
    tot += _send_all(g, core, T, topo, P)

    r = rank
    nst = 0
    if r >= 1:
        wid = CB * r
        if r >= 3:
            chunks = [(0, wid // 2), (wid // 2, wid)]
        else:
            chunks = [(0, wid)]
        others = sorted([i for i in range(len(P["cores"])) if i != r], key=lambda i: P["due"][(r, i)])
        order = [r] + others
        for n_, i in enumerate(order):
            if i == r:
                g.tensor.wait_ge(T.sem.ld, 16)
            else:
                g.tensor.wait_ge(T.sem["a%d" % i], P["expect"][(r, i)])
            lhsT = T.land[:, i * W + r * CB:i * W + (r + 1) * CB]
            for k, (a, b) in enumerate(chunks):
                g.tensor.matmul(T["ps%d" % k][:, 0:b - a], lhsT, T.land[:, i * W + a:i * W + b],
                                n_ == 0, n_ == len(order) - 1).then_inc(T.sem["mm%d" % k], 1)
        for k, (a, b) in enumerate(chunks):
            g.vector.wait_ge(T.sem["mm%d" % k], len(order))
            g.vector.tensor_copy(T.ysb[:, a:b], T["ps%d" % k][:, 0:b - a]).then_inc(T.sem["ev%d" % k], 1)
        for k, (a, b) in enumerate(chunks):
            q = g.sync if k == 0 else g.scalar
            q.wait_ge(T.sem["ev%d" % k], 1)
            q.dma_start(T.y[:, a:b], T.ysb[:, a:b]).then_inc(T.sem.st, 16)
            nst += 16

    g.wait_ge(T.sem.sent, tot)
    if nst:
        g.wait_ge(T.sem.st, nst)
